import numpy as np
import ml_dtypes


def mxq(x, axis, fmt="e4m3"):
    dtype, down = {"e4m3": (ml_dtypes.float8_e4m3fn, 7), "e5m2": (ml_dtypes.float8_e5m2, 14)}[fmt]
    v = np.moveaxis(np.asarray(x, np.float32).astype(ml_dtypes.bfloat16).astype(np.float64), axis, -1)
    blocks = v.reshape(v.shape[:-1] + (-1, 32))
    amax = np.abs(blocks).max(-1, keepdims=True)
    byte = np.maximum(np.where(amax > 0, np.frexp(amax)[1] - 1 + 127, 0) - down, 1)
    scale = np.exp2(byte - 127.0)
    codes = (blocks / scale).astype(np.float32).astype(dtype).astype(np.float64)
    return np.moveaxis((codes * scale).reshape(v.shape), -1, axis)


WIDE = False


def mx_kscale(k):
    if not WIDE:
        return np.ones(k)
    levels = np.array([10, -10, 5, -5, 0])
    if k % 512:
        return np.exp2(np.random.permutation(np.resize(levels, k // 32))).repeat(32)
    a = np.empty((k // 512, 16))
    for p in range(k // 512):
        a[p, :8] = np.random.permutation(np.resize(levels, 8))
        for g in range(8):
            far = levels[np.abs(levels - a[p, g]) >= 10]
            a[p, g + 8] = far[np.random.randint(len(far))]
    return np.exp2(a.ravel()).repeat(32)


def f64(x):
    return np.asarray(x).astype(np.float64)


def striped(idx):
    return np.tile(idx.reshape(-1, 16).T, (8, 1)).astype(np.uint16)


def unstriped(offs):
    return offs[:16].T.reshape(-1).astype(np.int64)


def pack_weight(w):
    k, n = w.shape
    w = f64(np.asarray(w, np.float32).astype(ml_dtypes.bfloat16)).reshape(k // 32, 32, n)
    amax = np.abs(w).max(1)
    byte = np.clip(np.where(amax > 0, np.frexp(amax)[1] - 1 + 127 - 7, 1), 1, 254)
    scaled = (w * np.exp2(127.0 - byte)[:, None, :]).reshape(k, n).astype(np.float32)
    words = np.ascontiguousarray(scaled.reshape(k // 512, 128, 4, n).transpose(0, 1, 3, 2)).astype(ml_dtypes.float8_e4m3fn).view(np.uint8)
    return words, np.ascontiguousarray(byte.astype(np.uint8).reshape(k // 512, 16, n))


def unpack_weight(words, scales):
    g, p, n, _ = words.shape
    vals = np.ascontiguousarray(words).view(ml_dtypes.float8_e4m3fn).astype(np.float64) * np.repeat(np.exp2(scales.astype(np.float64) - 127.0), 8, axis=1)[..., None]
    return vals.transpose(0, 1, 3, 2).reshape(g * 512, n)


E2M1 = np.array([0.0, 0.5, 1.0, 1.5, 2.0, 3.0, 4.0, 6.0, -0.0, -0.5, -1.0, -1.5, -2.0, -3.0, -4.0, -6.0])


def pack_fp4(w):
    k, n = w.shape
    w = f64(np.asarray(w, np.float32).astype(ml_dtypes.bfloat16)).reshape(k // 32, 32, n)
    amax = np.abs(w).max(1)
    mant, ex = np.frexp(amax / 6.0)
    byte = np.clip(np.where(amax > 0, np.where(mant > 0.5, ex, ex - 1) + 127, 1), 1, 254)
    scaled = (w * np.exp2(127.0 - byte)[:, None, :]).reshape(k, n).astype(np.float32)
    c = np.ascontiguousarray(scaled.reshape(k // 512, 128, 4, n).transpose(0, 1, 3, 2)).astype(ml_dtypes.float4_e2m1fn).view(np.uint8) & 0xF
    words = (c[..., 0::2] | (c[..., 1::2] << 4)).reshape(k // 512, 128, 2 * n)
    return np.ascontiguousarray(words), np.ascontiguousarray(byte.astype(np.uint8).reshape(k // 512, 16, n))


def unpack_fp4(words, scales):
    g, _, n = scales.shape
    words = np.ascontiguousarray(words).reshape(g, 128, n, 2)
    nib = np.empty((g, 128, n, 4), np.uint8)
    nib[..., 0::2] = words & 0xF
    nib[..., 1::2] = words >> 4
    vals = E2M1[nib] * np.repeat(np.exp2(scales.astype(np.float64) - 127.0), 8, axis=1)[..., None]
    return vals.transpose(0, 1, 3, 2).reshape(g * 512, n)


def sigmoid(v):
    return 1.0 / (1.0 + np.exp(-np.maximum(v, -700.0)))


K, T, S, D, N, H, V, U = 1024, 4096, 1024, 4, 256, 512, 256, 512


def setup_inputs():
    n = np.random.standard_normal
    s = mx_kscale(K)[:, None]
    u = mx_kscale(H)
    packed_xT = pack_weight(n((K, T)) * s)
    packed_w1 = pack_fp4(n((K, H)) / np.sqrt(K) / s)
    packed_w2 = pack_fp4(n((K, H)) / np.sqrt(K) / s)
    packed_w3 = pack_fp4(n((H, N)) / np.sqrt(H) / u[:, None])
    return {
        "x_words": packed_xT[0],
        "x_scales": packed_xT[1],
        "w1_words": packed_w1[0],
        "w1_scales": packed_w1[1],
        "w2_words": packed_w2[0],
        "w2_scales": packed_w2[1],
        "unit": (np.random.uniform(0.6, 1.4, (H, 1)) * u[:, None]).astype(np.float32),
        "w3_words": packed_w3[0],
        "w3_scales": packed_w3[1],
        "offs": striped(np.random.permutation(T)[:S]),
        "va": striped(np.random.permutation(np.concatenate([np.arange(V), np.random.randint(0, V, U - V)]))),
        "vb2": striped(np.random.permutation(np.concatenate([np.arange(V), np.random.randint(0, V, U - V)]))),
    }


def reference(x_words, x_scales, w1_words, w1_scales, w2_words, w2_scales, unit, w3_words, w3_scales, offs, va, vb2):
    xq = unpack_weight(x_words, x_scales)[:, unstriped(offs)]
    y = unpack_fp4(w1_words, w1_scales).T @ xq
    yv = unpack_fp4(w2_words, w2_scales).T @ xq
    visi = sigmoid(2.0 * yv)
    yl = y * visi
    direct = yl.reshape(len(yl), -1, D).sum(axis=2)
    la = direct[:, unstriped(va)]
    open_ = visi.reshape(len(visi), -1, D).mean(axis=2)
    aa = open_[:, unstriped(va)]
    lb = direct[:, unstriped(vb2)]
    bounce = la + 0.8 * ((-1.0 * aa + 1.0) * lb)
    hid = f64(unit) * (np.log(np.abs(bounce) + 0.3))
    return unpack_fp4(w3_words, w3_scales).T @ mxq(hid, 0, "e4m3")

@@ -1,0 +1,245 @@
+from contextlib import ExitStack
+
+import concourse.mybir as mybir
+
+K, T, S, D, N, H, V, U = 1024, 4096, 1024, 4, 256, 512, 256, 512
+FLOPS = 2 * (2 * K * H * S + H * N * U)
+
+F32 = mybir.dt.float32
+BF16 = mybir.dt.bfloat16
+I32 = mybir.dt.int32
+U32 = mybir.dt.uint32
+U16 = mybir.dt.uint16
+U8 = mybir.dt.uint8
+FP8X4 = mybir.dt.float8_e4m3fn_x4
+FP4X4 = mybir.dt.float4_e2m1fn_x4
+ACT = mybir.ActivationFunctionType
+ALU = mybir.AluOpType
+
+P = 128
+PACK = 4
+PASSES = K // (P * PACK)
+HALF = S // 2
+VH = HALF // D
+ORDER = (((0, 0), (0, 1), (1, 0), (1, 1)), ((0, 2), (1, 2), (0, 3), (1, 3)))
+CHUNKS = ((0, 256), (256, 384), (384, 512))
+SCALAR_C = (0, 1)
+
+
+def tile_picked_yprtrn_log_p_kernel(
+    tc, x_words, x_scales, w1_words, w1_scales, w2_words, w2_scales, unit, w3_words, w3_scales, offs, va, vb2, out
+):
+    nc = tc.nc
+    with ExitStack() as ctx:
+        keep = ctx.enter_context(tc.tile_pool(name="keep", bufs=1))
+        ring = ctx.enter_context(tc.tile_pool(name="ring", bufs=3))
+        psum = ctx.enter_context(tc.psum_pool(name="psum", bufs=8))
+
+        offs_t = keep.tile([P, S // 16], U16, name="offs_t")
+        va_t = keep.tile([P, U // 16], U16, name="va_t")
+        vb_t = keep.tile([P, U // 16], U16, name="vb_t")
+        nc.sync.dma_start(offs_t[:], offs)
+
+        xs_win = keep.tile([P, T], U8, name="xs_win", align_bytes=64)
+        nc.gpsimd.memset(xs_win[:, : T // 2].bitcast(I32), 0)
+        nc.vector.memset(xs_win[:, T // 2 :].bitcast(I32), 0)
+        xs_rows = x_scales.bitcast(I32).rearrange("g (q r) c -> r q g c", r=4)
+        for r in range(4):
+            nc.sync.dma_start(out=xs_win[r:P:16, :].bitcast(I32), in_=xs_rows[r])
+
+        w_raw = [keep.tile([P, PASSES, 2 * H], U8, name=f"w_raw{j}", align_bytes=64) for j in range(2)]
+        ws_raw = [keep.tile([P, PASSES, H], U8, name=f"ws_raw{j}", align_bytes=64) for j in range(2)]
+        x_win = [keep.tile([P, T], U32, name=f"x_win{g}", align_bytes=64) for g in range(PASSES)]
+
+        def load_words(j, words):
+            nc.sync.dma_start(out=w_raw[j][:].bitcast(I32), in_=words.bitcast(I32).rearrange("g p c -> p g c"))
+
+        def load_scales(j, scales):
+            nc.vector.memset(ws_raw[j][:].bitcast(I32), 0)
+            for q in range(4):
+                nc.sync.dma_start(
+                    out=ws_raw[j][32 * q : 32 * q + 4].bitcast(I32),
+                    in_=scales.bitcast(I32)[:, 4 * q : 4 * q + 4, :].rearrange("g r c -> r g c"),
+                )
+
+        def load_x(g, part):
+            cols = slice(part * T // 2, (part + 1) * T // 2)
+            src = x_words[g].rearrange("p n t -> p (n t)").bitcast(I32)
+            nc.sync.dma_start(out=x_win[g][:, cols].bitcast(I32), in_=src[:, cols])
+
+        load_words(0, w2_words)
+        load_words(1, w1_words)
+        load_x(0, 0)
+        load_x(0, 1)
+        load_scales(0, w2_scales)
+        load_x(1, 0)
+        load_scales(1, w1_scales)
+        load_x(1, 1)
+
+        nc.sync.dma_start(va_t[:], va)
+        nc.sync.dma_start(vb_t[:], vb2)
+        unit_t = keep.tile([P, PACK], F32, name="unit_t")
+        nc.sync.dma_start(out=unit_t[:], in_=unit.rearrange("(p t) o -> p (t o)", t=PACK))
+        w3_t = keep.tile([P, 2 * N], U8, name="w3_t", align_bytes=64)
+        nc.sync.dma_start(out=w3_t[:].bitcast(I32), in_=w3_words[0].bitcast(I32))
+        w3s_t = keep.tile([P, N], U8, name="w3s_t", align_bytes=64)
+        nc.gpsimd.memset(w3s_t[:].bitcast(I32), 0)
+        for q in range(4):
+            nc.sync.dma_start(
+                out=w3s_t[32 * q : 32 * q + 4, :].bitcast(I32), in_=w3_scales[0].bitcast(I32)[4 * q : 4 * q + 4, :]
+            )
+
+        xs_g = keep.tile([P, S], U8, name="xs_g", align_bytes=64)
+        nc.vector.tensor_copy(xs_g[:], xs_win[:].indirect(offs_t[:]))
+        xs_1 = keep.tile([P, S], U8, name="xs_1", align_bytes=64)
+        nc.gpsimd.memset(xs_1[:].bitcast(I32), 0)
+        nc.gpsimd.dma_start(out=xs_1[0:112, :].bitcast(I32), in_=xs_g[16:P, :].bitcast(I32))
+        xs_plane = [xs_g, xs_1]
+
+        def deal(j):
+            words = keep.tile([P, PASSES, 2 * H], U8, name=f"w_deal{j}", align_bytes=64)
+            nc.vector.tensor_copy(
+                out=words[:].rearrange("p g (t m b) -> p g t m b", t=PACK, b=2),
+                in_=w_raw[j][:].rearrange("p g (m t b) -> p g t m b", t=PACK, b=2),
+            )
+            scales = keep.tile([P, PASSES, H], U8, name=f"ws_deal{j}", align_bytes=64)
+            nc.vector.tensor_copy(
+                out=scales[:].rearrange("p g (t m) -> p g t m", t=PACK),
+                in_=ws_raw[j][:].rearrange("p g (m t) -> p g t m", t=PACK),
+            )
+            return words, scales
+
+        xg = {}
+
+        def gather_x(g, h):
+            tile = keep.tile([P, HALF], U32, name=f"xg{g}{h}", align_bytes=64)
+            cols = HALF // 16
+            nc.vector.tensor_copy(tile[:], x_win[g][:].indirect(offs_t[:, h * cols : (h + 1) * cols]))
+            xg[g, h] = tile
+
+        w_dealt = [deal(0)]
+        gather_x(0, 0)
+        w_dealt.append(deal(1))
+        gather_x(0, 1)
+        gather_x(1, 0)
+        gather_x(1, 1)
+
+        def mx_pass(acc, j, t, h, g):
+            words, scales = w_dealt[j]
+            nc.tensor.matmul_mx(
+                out=acc[:],
+                lhsT=words[:, g, 2 * P * t : 2 * P * (t + 1)].bitcast(FP4X4),
+                lhsT_scale=scales[:, g, P * t : P * (t + 1)],
+                rhs=xg[g, h][:].bitcast(FP8X4),
+                rhs_scale=xs_plane[g][:, h * HALF : (h + 1) * HALF],
+                start=(g == 0),
+                stop=(g == PASSES - 1),
+            )
+
+        shut = [keep.tile([P, D, V], F32, name=f"shut{t}") for t in range(PACK)]
+        lit = [keep.tile([P, D, V], F32, name=f"lit{t}") for t in range(PACK)]
+        dir_t = [keep.tile([P, 3 * V], F32, name=f"dir{t}") for t in range(PACK)]
+        clo_t = [keep.tile([P, 3 * V], F32, name=f"clo{t}") for t in range(PACK)]
+
+        def gate(t, h, acc_v, acc_y):
+            vs = slice(h * VH, (h + 1) * VH)
+            nc.scalar.activation(
+                out=shut[t][:, :, vs], in_=acc_v[:].rearrange("p (v d) -> p d v", d=D), func=ACT.Sigmoid, scale=-2.0
+            )
+            pair = clo_t[t][:, V:].rearrange("p (d v) -> p d v", d=2)
+            nc.gpsimd.tensor_tensor(pair[:, :, vs], shut[t][:, 0:2, vs], shut[t][:, 2:4, vs], ALU.add)
+            nc.vector.scalar_tensor_tensor(
+                out=lit[t][:, :, vs],
+                in0=shut[t][:, :, vs],
+                scalar=1.0,
+                in1=acc_y[:].rearrange("p (v d) -> p d v", d=D),
+                op0=ALU.subtract,
+                op1=ALU.mult,
+            )
+
+        def sums(t):
+            pairs = ((dir_t[t], lit[t]), (clo_t[t], shut[t]))
+            for table, src in pairs[:1]:
+                flat = src[:].rearrange("p d v -> p (d v)")
+                nc.vector.tensor_tensor(table[:, V:], flat[:, : 2 * V], flat[:, 2 * V :], ALU.add)
+            for table, src in pairs[::-1]:
+                nc.vector.tensor_tensor(table[:, :V], table[:, V : 2 * V], table[:, 2 * V :], ALU.add)
+
+        for tp in range(2):
+            ts = (2 * tp, 2 * tp + 1)
+            accs = {}
+            steps = [(g, h, t, j) for g in range(PASSES) for h, t in ORDER[tp] for j in range(2)]
+            if tp == 1:
+                steps = [(g, h, t, j) for h, t in ORDER[tp] for j in range(2) for g in range(PASSES)]
+            for g, h, t, j in steps:
+                if g == 0:
+                    accs[t, h, j] = psum.tile([P, HALF], F32, name="acc")
+                mx_pass(accs[t, h, j], j, t, h, g)
+            for h, t in ORDER[tp]:
+                if True:
+                    gate(t, h, accs[t, h, 0], accs[t, h, 1])
+        for t in range(PACK):
+            sums(t)
+
+        mag = keep.tile([P, PACK, U], F32, name="mag")
+        logs = keep.tile([P, PACK, U], F32, name="logs")
+
+        def bounce(t, r0, r1):
+            n = r1 - r0
+            ia = va_t[:, r0 // 16 : r1 // 16]
+            ib = vb_t[:, r0 // 16 : r1 // 16]
+            other = ring.tile([P, n], F32, name="other")
+            nc.scalar.activation(out=other[:], in_=dir_t[t][:].indirect(ib), func=ACT.Copy, scale=0.2)
+            extra = ring.tile([P, n], F32, name="extra")
+            if t in SCALAR_C:
+                closed = ring.tile([P, n], F32, name="closed")
+                nc.scalar.activation(out=closed[:], in_=clo_t[t][:].indirect(ia), func=ACT.Copy)
+                nc.vector.tensor_tensor(extra[:], closed[:], other[:], ALU.mult)
+            else:
+                nc.vector.tensor_tensor(extra[:], clo_t[t][:].indirect(ia), other[:], ALU.mult)
+            total = ring.tile([P, n], F32, name="total")
+            nc.vector.tensor_tensor(total[:], dir_t[t][:].indirect(ia), extra[:], ALU.add)
+            nc.scalar.activation(out=mag[:, t, r0:r1], in_=total[:], func=ACT.Abs)
+
+        def log_of(t, r0, r1):
+            nc.scalar.activation(out=logs[:, t, r0:r1], in_=mag[:, t, r0:r1], func=ACT.Ln, bias=0.3)
+
+        def finish(rh, r1):
+            RH = r1 - rh
+            rs = slice(rh, r1)
+            hid = keep.tile([P, RH, PACK], BF16, name=f"hid{rh}", align_bytes=64)
+            nc.vector.tensor_tensor(
+                hid[:].rearrange("p (c i) t -> p c t i", i=4),
+                logs[:, :, rs].rearrange("p t (c i) -> p c t i", i=4),
+                unit_t[:].unsqueeze(1).unsqueeze(3).to_broadcast([P, RH // 4, PACK, 4]),
+                ALU.mult,
+            )
+            codes = keep.tile([P, RH], U32, name=f"codes{rh}", align_bytes=64)
+            plane = keep.tile([P, RH], U8, name=f"plane{rh}", align_bytes=64)
+            nc.vector.quantize_mx(
+                out=codes[:].bitcast(FP8X4), scales=plane[:], in_=hid[:].rearrange("p r t -> p (r t)")
+            )
+            acc = psum.tile([P, HALF], F32, name="acc")
+            for a in range(N // P):
+                nc.tensor.matmul_mx(
+                    out=acc[:, a * RH : (a + 1) * RH],
+                    lhsT=w3_t[:, 2 * P * a : 2 * P * (a + 1)].bitcast(FP4X4),
+                    lhsT_scale=w3s_t[:, P * a : P * (a + 1)],
+                    rhs=codes[:].bitcast(FP8X4),
+                    rhs_scale=plane[:],
+                    start=True,
+                    stop=True,
+                )
+            res = keep.tile([P, N // P, RH], F32, name=f"res{rh}")
+            nc.scalar.copy(out=res[:].rearrange("p a r -> p (a r)"), in_=acc[:, : 2 * RH])
+            nc.sync.dma_start(out=out.rearrange("(a p) r -> p a r", p=P)[:, :, rs], in_=res[:])
+
+        for t in range(PACK - 1):
+            bounce(t, 0, U)
+        for t in range(PACK - 1):
+            log_of(t, 0, U)
+        for r0, r1 in CHUNKS:
+            bounce(PACK - 1, r0, r1)
+            log_of(PACK - 1, r0, r1)
+        for r0, r1 in CHUNKS:
+            finish(r0, r1)

@@ -70,10 +70,10 @@ def tile_picked_yprtrn_log_p_kernel(
         load_words(0, w2_words)
         load_words(1, w1_words)
         load_x(0, 0)
-        load_x(0, 1)
         load_scales(0, w2_scales)
-        load_x(1, 0)
+        load_x(0, 1)
         load_scales(1, w1_scales)
+        load_x(1, 0)
         load_x(1, 1)
 
         nc.sync.dma_start(va_t[:], va)
@@ -183,8 +183,10 @@ def tile_picked_yprtrn_log_p_kernel(
 
         mag = keep.tile([P, PACK, U], F32, name="mag")
         logs = keep.tile([P, PACK, U], F32, name="logs")
+        hid_rows = keep.tile([P, PACK, U], BF16, name="hid_rows")
+        extras = {}
 
-        def bounce(t, r0, r1):
+        def second_light(t, r0, r1):
             n = r1 - r0
             ia = va_t[:, r0 // 16 : r1 // 16]
             ib = vb_t[:, r0 // 16 : r1 // 16]
@@ -197,32 +199,39 @@ def tile_picked_yprtrn_log_p_kernel(
                 nc.vector.tensor_tensor(extra[:], closed[:], other[:], ALU.mult)
             else:
                 nc.vector.tensor_tensor(extra[:], clo_t[t][:].indirect(ia), other[:], ALU.mult)
-            total = ring.tile([P, n], F32, name="total")
-            nc.vector.tensor_tensor(total[:], dir_t[t][:].indirect(ia), extra[:], ALU.add)
+            extras[t, r0] = extra
+
+        def bounce(t, r0, r1):
+            ia = va_t[:, r0 // 16 : r1 // 16]
+            total = ring.tile([P, r1 - r0], F32, name="total")
+            nc.vector.tensor_tensor(total[:], dir_t[t][:].indirect(ia), extras[t, r0][:], ALU.add)
             nc.scalar.activation(out=mag[:, t, r0:r1], in_=total[:], func=ACT.Abs)
 
         def log_of(t, r0, r1):
             nc.scalar.activation(out=logs[:, t, r0:r1], in_=mag[:, t, r0:r1], func=ACT.Ln, bias=0.3)
+            nc.vector.tensor_scalar_mul(hid_rows[:, t, r0:r1], logs[:, t, r0:r1], unit_t[:, t : t + 1])
 
-        def finish(rh, r1):
-            RH = r1 - rh
-            rs = slice(rh, r1)
-            hid = keep.tile([P, RH, PACK], BF16, name=f"hid{rh}", align_bytes=64)
-            nc.vector.tensor_tensor(
+        hids = {}
+
+        def weave(r0, r1):
+            hid = keep.tile([P, r1 - r0, PACK], BF16, name=f"hid{r0}", align_bytes=64)
+            nc.vector.tensor_copy(
                 hid[:].rearrange("p (c i) t -> p c t i", i=4),
-                logs[:, :, rs].rearrange("p t (c i) -> p c t i", i=4),
-                unit_t[:].unsqueeze(1).unsqueeze(3).to_broadcast([P, RH // 4, PACK, 4]),
-                ALU.mult,
+                hid_rows[:, :, r0:r1].rearrange("p t (c i) -> p c t i", i=4),
             )
-            codes = keep.tile([P, RH], U32, name=f"codes{rh}", align_bytes=64)
-            plane = keep.tile([P, RH], U8, name=f"plane{rh}", align_bytes=64)
+            hids[r0] = hid
+
+        def finish(r0, r1):
+            n = r1 - r0
+            codes = keep.tile([P, n], U32, name=f"codes{r0}", align_bytes=64)
+            plane = keep.tile([P, n], U8, name=f"plane{r0}", align_bytes=64)
             nc.vector.quantize_mx(
-                out=codes[:].bitcast(FP8X4), scales=plane[:], in_=hid[:].rearrange("p r t -> p (r t)")
+                out=codes[:].bitcast(FP8X4), scales=plane[:], in_=hids[r0][:].rearrange("p r t -> p (r t)")
             )
             acc = psum.tile([P, HALF], F32, name="acc")
             for a in range(N // P):
                 nc.tensor.matmul_mx(
-                    out=acc[:, a * RH : (a + 1) * RH],
+                    out=acc[:, a * n : (a + 1) * n],
                     lhsT=w3_t[:, 2 * P * a : 2 * P * (a + 1)].bitcast(FP4X4),
                     lhsT_scale=w3s_t[:, P * a : P * (a + 1)],
                     rhs=codes[:].bitcast(FP8X4),
@@ -230,16 +239,20 @@ def tile_picked_yprtrn_log_p_kernel(
                     start=True,
                     stop=True,
                 )
-            res = keep.tile([P, N // P, RH], F32, name=f"res{rh}")
-            nc.scalar.copy(out=res[:].rearrange("p a r -> p (a r)"), in_=acc[:, : 2 * RH])
-            nc.sync.dma_start(out=out.rearrange("(a p) r -> p a r", p=P)[:, :, rs], in_=res[:])
+            res = keep.tile([P, N // P, n], F32, name=f"res{r0}")
+            nc.scalar.copy(out=res[:].rearrange("p a r -> p (a r)"), in_=acc[:, : 2 * n])
+            nc.sync.dma_start(out=out.rearrange("(a p) r -> p a r", p=P)[:, :, r0:r1], in_=res[:])
 
-        for t in range(PACK - 1):
-            bounce(t, 0, U)
-        for t in range(PACK - 1):
-            log_of(t, 0, U)
-        for r0, r1 in CHUNKS:
-            bounce(PACK - 1, r0, r1)
-            log_of(PACK - 1, r0, r1)
-        for r0, r1 in CHUNKS:
-            finish(r0, r1)
+        units = [(t, 0, U) for t in range(PACK - 1)] + [(PACK - 1, r0, r1) for r0, r1 in CHUNKS]
+        for i in range(len(units) + 2):
+            if i < len(units):
+                second_light(*units[i])
+            if 1 <= i <= len(units):
+                bounce(*units[i - 1])
+            if i >= 2:
+                log_of(*units[i - 2])
+        for i in range(len(CHUNKS) + 1):
+            if i < len(CHUNKS):
+                weave(*CHUNKS[i])
+            if i >= 1:
+                finish(*CHUNKS[i - 1])

from contextlib import ExitStack

import concourse.mybir as mybir

K, T, S, D, N, H, V, U = 1024, 4096, 1024, 4, 256, 512, 256, 512
FLOPS = 2 * (2 * K * H * S + H * N * U)

F32 = mybir.dt.float32
BF16 = mybir.dt.bfloat16
I32 = mybir.dt.int32
U32 = mybir.dt.uint32
U16 = mybir.dt.uint16
U8 = mybir.dt.uint8
FP8X4 = mybir.dt.float8_e4m3fn_x4
FP4X4 = mybir.dt.float4_e2m1fn_x4
ACT = mybir.ActivationFunctionType
ALU = mybir.AluOpType

P = 128
PACK = 4
PASSES = K // (P * PACK)
HALF = S // 2
VH = HALF // D
ORDER = (((0, 0), (0, 1), (1, 0), (1, 1)), ((0, 2), (1, 2), (0, 3), (1, 3)))
CHUNKS = ((0, 256), (256, 384), (384, 512))
SCALAR_C = (0, 1)


def tile_picked_yprtrn_log_p_kernel(
    tc, x_words, x_scales, w1_words, w1_scales, w2_words, w2_scales, unit, w3_words, w3_scales, offs, va, vb2, out
):
    nc = tc.nc
    with ExitStack() as ctx:
        keep = ctx.enter_context(tc.tile_pool(name="keep", bufs=1))
        ring = ctx.enter_context(tc.tile_pool(name="ring", bufs=3))
        psum = ctx.enter_context(tc.psum_pool(name="psum", bufs=8))

        offs_t = keep.tile([P, S // 16], U16, name="offs_t")
        va_t = keep.tile([P, U // 16], U16, name="va_t")
        vb_t = keep.tile([P, U // 16], U16, name="vb_t")
        nc.sync.dma_start(offs_t[:], offs)

        xs_win = keep.tile([P, T], U8, name="xs_win", align_bytes=64)
        nc.gpsimd.memset(xs_win[:, : T // 2].bitcast(I32), 0)
        nc.vector.memset(xs_win[:, T // 2 :].bitcast(I32), 0)
        xs_rows = x_scales.bitcast(I32).rearrange("g (q r) c -> r q g c", r=4)
        for r in range(4):
            nc.sync.dma_start(out=xs_win[r:P:16, :].bitcast(I32), in_=xs_rows[r])

        w_raw = [keep.tile([P, PASSES, 2 * H], U8, name=f"w_raw{j}", align_bytes=64) for j in range(2)]
        ws_raw = [keep.tile([P, PASSES, H], U8, name=f"ws_raw{j}", align_bytes=64) for j in range(2)]
        x_win = [keep.tile([P, T], U32, name=f"x_win{g}", align_bytes=64) for g in range(PASSES)]

        def load_words(j, words):
            nc.sync.dma_start(out=w_raw[j][:].bitcast(I32), in_=words.bitcast(I32).rearrange("g p c -> p g c"))

        def load_scales(j, scales):
            nc.vector.memset(ws_raw[j][:].bitcast(I32), 0)
            for q in range(4):
                nc.sync.dma_start(
                    out=ws_raw[j][32 * q : 32 * q + 4].bitcast(I32),
                    in_=scales.bitcast(I32)[:, 4 * q : 4 * q + 4, :].rearrange("g r c -> r g c"),
                )

        def load_x(g, part):
            cols = slice(part * T // 2, (part + 1) * T // 2)
            src = x_words[g].rearrange("p n t -> p (n t)").bitcast(I32)
            nc.sync.dma_start(out=x_win[g][:, cols].bitcast(I32), in_=src[:, cols])

        load_words(0, w2_words)
        load_words(1, w1_words)
        load_x(0, 0)
        load_scales(0, w2_scales)
        load_x(0, 1)
        load_scales(1, w1_scales)
        load_x(1, 0)
        load_x(1, 1)

        nc.sync.dma_start(va_t[:], va)
        nc.sync.dma_start(vb_t[:], vb2)
        unit_t = keep.tile([P, PACK], F32, name="unit_t")
        nc.sync.dma_start(out=unit_t[:], in_=unit.rearrange("(p t) o -> p (t o)", t=PACK))
        w3_t = keep.tile([P, 2 * N], U8, name="w3_t", align_bytes=64)
        nc.sync.dma_start(out=w3_t[:].bitcast(I32), in_=w3_words[0].bitcast(I32))
        w3s_t = keep.tile([P, N], U8, name="w3s_t", align_bytes=64)
        nc.gpsimd.memset(w3s_t[:].bitcast(I32), 0)
        for q in range(4):
            nc.sync.dma_start(
                out=w3s_t[32 * q : 32 * q + 4, :].bitcast(I32), in_=w3_scales[0].bitcast(I32)[4 * q : 4 * q + 4, :]
            )

        xs_g = keep.tile([P, S], U8, name="xs_g", align_bytes=64)
        nc.vector.tensor_copy(xs_g[:], xs_win[:].indirect(offs_t[:]))
        xs_1 = keep.tile([P, S], U8, name="xs_1", align_bytes=64)
        nc.gpsimd.memset(xs_1[:].bitcast(I32), 0)
        nc.gpsimd.dma_start(out=xs_1[0:112, :].bitcast(I32), in_=xs_g[16:P, :].bitcast(I32))
        xs_plane = [xs_g, xs_1]

        def deal(j):
            words = keep.tile([P, PASSES, 2 * H], U8, name=f"w_deal{j}", align_bytes=64)
            nc.vector.tensor_copy(
                out=words[:].rearrange("p g (t m b) -> p g t m b", t=PACK, b=2),
                in_=w_raw[j][:].rearrange("p g (m t b) -> p g t m b", t=PACK, b=2),
            )
            scales = keep.tile([P, PASSES, H], U8, name=f"ws_deal{j}", align_bytes=64)
            nc.vector.tensor_copy(
                out=scales[:].rearrange("p g (t m) -> p g t m", t=PACK),
                in_=ws_raw[j][:].rearrange("p g (m t) -> p g t m", t=PACK),
            )
            return words, scales

        xg = {}

        def gather_x(g, h):
            tile = keep.tile([P, HALF], U32, name=f"xg{g}{h}", align_bytes=64)
            cols = HALF // 16
            nc.vector.tensor_copy(tile[:], x_win[g][:].indirect(offs_t[:, h * cols : (h + 1) * cols]))
            xg[g, h] = tile

        w_dealt = [deal(0)]
        gather_x(0, 0)
        w_dealt.append(deal(1))
        gather_x(0, 1)
        gather_x(1, 0)
        gather_x(1, 1)

        def mx_pass(acc, j, t, h, g):
            words, scales = w_dealt[j]
            nc.tensor.matmul_mx(
                out=acc[:],
                lhsT=words[:, g, 2 * P * t : 2 * P * (t + 1)].bitcast(FP4X4),
                lhsT_scale=scales[:, g, P * t : P * (t + 1)],
                rhs=xg[g, h][:].bitcast(FP8X4),
                rhs_scale=xs_plane[g][:, h * HALF : (h + 1) * HALF],
                start=(g == 0),
                stop=(g == PASSES - 1),
            )

        shut = [keep.tile([P, D, V], F32, name=f"shut{t}") for t in range(PACK)]
        lit = [keep.tile([P, D, V], F32, name=f"lit{t}") for t in range(PACK)]
        dir_t = [keep.tile([P, 3 * V], F32, name=f"dir{t}") for t in range(PACK)]
        clo_t = [keep.tile([P, 3 * V], F32, name=f"clo{t}") for t in range(PACK)]

        def gate(t, h, acc_v, acc_y):
            vs = slice(h * VH, (h + 1) * VH)
            nc.scalar.activation(
                out=shut[t][:, :, vs], in_=acc_v[:].rearrange("p (v d) -> p d v", d=D), func=ACT.Sigmoid, scale=-2.0
            )
            pair = clo_t[t][:, V:].rearrange("p (d v) -> p d v", d=2)
            nc.gpsimd.tensor_tensor(pair[:, :, vs], shut[t][:, 0:2, vs], shut[t][:, 2:4, vs], ALU.add)
            nc.vector.scalar_tensor_tensor(
                out=lit[t][:, :, vs],
                in0=shut[t][:, :, vs],
                scalar=1.0,
                in1=acc_y[:].rearrange("p (v d) -> p d v", d=D),
                op0=ALU.subtract,
                op1=ALU.mult,
            )

        def sums(t):
            pairs = ((dir_t[t], lit[t]), (clo_t[t], shut[t]))
            for table, src in pairs[:1]:
                flat = src[:].rearrange("p d v -> p (d v)")
                nc.vector.tensor_tensor(table[:, V:], flat[:, : 2 * V], flat[:, 2 * V :], ALU.add)
            for table, src in pairs[::-1]:
                nc.vector.tensor_tensor(table[:, :V], table[:, V : 2 * V], table[:, 2 * V :], ALU.add)

        for tp in range(2):
            ts = (2 * tp, 2 * tp + 1)
            accs = {}
            steps = [(g, h, t, j) for g in range(PASSES) for h, t in ORDER[tp] for j in range(2)]
            if tp == 1:
                steps = [(g, h, t, j) for h, t in ORDER[tp] for j in range(2) for g in range(PASSES)]
            for g, h, t, j in steps:
                if g == 0:
                    accs[t, h, j] = psum.tile([P, HALF], F32, name="acc")
                mx_pass(accs[t, h, j], j, t, h, g)
            for h, t in ORDER[tp]:
                if True:
                    gate(t, h, accs[t, h, 0], accs[t, h, 1])
        for t in range(PACK):
            sums(t)

        mag = keep.tile([P, PACK, U], F32, name="mag")
        logs = keep.tile([P, PACK, U], F32, name="logs")
        hid_rows = keep.tile([P, PACK, U], BF16, name="hid_rows")
        extras = {}

        def second_light(t, r0, r1):
            n = r1 - r0
            ia = va_t[:, r0 // 16 : r1 // 16]
            ib = vb_t[:, r0 // 16 : r1 // 16]
            other = ring.tile([P, n], F32, name="other")
            nc.scalar.activation(out=other[:], in_=dir_t[t][:].indirect(ib), func=ACT.Copy, scale=0.2)
            extra = ring.tile([P, n], F32, name="extra")
            if t in SCALAR_C:
                closed = ring.tile([P, n], F32, name="closed")
                nc.scalar.activation(out=closed[:], in_=clo_t[t][:].indirect(ia), func=ACT.Copy)
                nc.vector.tensor_tensor(extra[:], closed[:], other[:], ALU.mult)
            else:
                nc.vector.tensor_tensor(extra[:], clo_t[t][:].indirect(ia), other[:], ALU.mult)
            extras[t, r0] = extra

        def bounce(t, r0, r1):
            ia = va_t[:, r0 // 16 : r1 // 16]
            total = ring.tile([P, r1 - r0], F32, name="total")
            nc.vector.tensor_tensor(total[:], dir_t[t][:].indirect(ia), extras[t, r0][:], ALU.add)
            nc.scalar.activation(out=mag[:, t, r0:r1], in_=total[:], func=ACT.Abs)

        def log_of(t, r0, r1):
            nc.scalar.activation(out=logs[:, t, r0:r1], in_=mag[:, t, r0:r1], func=ACT.Ln, bias=0.3)
            nc.vector.tensor_scalar_mul(hid_rows[:, t, r0:r1], logs[:, t, r0:r1], unit_t[:, t : t + 1])

        hids = {}

        def weave(r0, r1):
            hid = keep.tile([P, r1 - r0, PACK], BF16, name=f"hid{r0}", align_bytes=64)
            nc.vector.tensor_copy(
                hid[:].rearrange("p (c i) t -> p c t i", i=4),
                hid_rows[:, :, r0:r1].rearrange("p t (c i) -> p c t i", i=4),
            )
            hids[r0] = hid

        def finish(r0, r1):
            n = r1 - r0
            codes = keep.tile([P, n], U32, name=f"codes{r0}", align_bytes=64)
            plane = keep.tile([P, n], U8, name=f"plane{r0}", align_bytes=64)
            nc.vector.quantize_mx(
                out=codes[:].bitcast(FP8X4), scales=plane[:], in_=hids[r0][:].rearrange("p r t -> p (r t)")
            )
            acc = psum.tile([P, HALF], F32, name="acc")
            for a in range(N // P):
                nc.tensor.matmul_mx(
                    out=acc[:, a * n : (a + 1) * n],
                    lhsT=w3_t[:, 2 * P * a : 2 * P * (a + 1)].bitcast(FP4X4),
                    lhsT_scale=w3s_t[:, P * a : P * (a + 1)],
                    rhs=codes[:].bitcast(FP8X4),
                    rhs_scale=plane[:],
                    start=True,
                    stop=True,
                )
            res = keep.tile([P, N // P, n], F32, name=f"res{r0}")
            nc.scalar.copy(out=res[:].rearrange("p a r -> p (a r)"), in_=acc[:, : 2 * n])
            nc.sync.dma_start(out=out.rearrange("(a p) r -> p a r", p=P)[:, :, r0:r1], in_=res[:])

        units = [(t, 0, U) for t in range(PACK - 1)] + [(PACK - 1, r0, r1) for r0, r1 in CHUNKS]
        for i in range(len(units) + 2):
            if i < len(units):
                second_light(*units[i])
            if 1 <= i <= len(units):
                bounce(*units[i - 1])
            if i >= 2:
                log_of(*units[i - 2])
        for i in range(len(CHUNKS) + 1):
            if i < len(CHUNKS):
                weave(*CHUNKS[i])
            if i >= 1:
                finish(*CHUNKS[i - 1])
